import numpy as np
import ml_dtypes


def mxq(x, axis, fmt="e4m3"):
    dtype, down = {"e4m3": (ml_dtypes.float8_e4m3fn, 7), "e5m2": (ml_dtypes.float8_e5m2, 14)}[fmt]
    v = np.moveaxis(np.asarray(x, np.float32).astype(ml_dtypes.bfloat16).astype(np.float64), axis, -1)
    blocks = v.reshape(v.shape[:-1] + (-1, 32))
    amax = np.abs(blocks).max(-1, keepdims=True)
    byte = np.maximum(np.where(amax > 0, np.frexp(amax)[1] - 1 + 127, 0) - down, 1)
    scale = np.exp2(byte - 127.0)
    codes = (blocks / scale).astype(np.float32).astype(dtype).astype(np.float64)
    return np.moveaxis((codes * scale).reshape(v.shape), -1, axis)


WIDE = False


def mx_kscale(k):
    if not WIDE:
        return np.ones(k)
    levels = np.array([10, -10, 5, -5, 0])
    if k % 512:
        return np.exp2(np.random.permutation(np.resize(levels, k // 32))).repeat(32)
    a = np.empty((k // 512, 16))
    for p in range(k // 512):
        a[p, :8] = np.random.permutation(np.resize(levels, 8))
        for g in range(8):
            far = levels[np.abs(levels - a[p, g]) >= 10]
            a[p, g + 8] = far[np.random.randint(len(far))]
    return np.exp2(a.ravel()).repeat(32)


def f64(x):
    return np.asarray(x).astype(np.float64)


def striped(idx):
    return np.tile(idx.reshape(-1, 16).T, (8, 1)).astype(np.uint16)


def unstriped(offs):
    return offs[:16].T.reshape(-1).astype(np.int64)


E2M1 = np.array([0.0, 0.5, 1.0, 1.5, 2.0, 3.0, 4.0, 6.0, -0.0, -0.5, -1.0, -1.5, -2.0, -3.0, -4.0, -6.0])


def pack_weight(w, fmt):
    k, n = w.shape
    w = f64(np.asarray(w, np.float32).astype(ml_dtypes.bfloat16)).reshape(k // 32, 32, n)
    amax = np.abs(w).max(1)
    if fmt == "e4m3":
        byte = np.frexp(amax)[1] - 1 + 127 - 7
    else:
        mant, ex = np.frexp(amax / 6.0)
        byte = np.where(mant > 0.5, ex, ex - 1) + 127
    byte = np.clip(np.where(amax > 0, byte, 1), 1, 254)
    scaled = (w * np.exp2(127.0 - byte)[:, None, :]).reshape(k, n).astype(np.float32)
    by_word = np.ascontiguousarray(scaled.reshape(k // 512, 128, 4, n).transpose(0, 1, 3, 2))
    if fmt == "e4m3":
        words = by_word.astype(ml_dtypes.float8_e4m3fn).view(np.uint8)
    else:
        c = by_word.astype(ml_dtypes.float4_e2m1fn).view(np.uint8) & 0xF
        words = (c[..., 0::2] | (c[..., 1::2] << 4)).reshape(k // 512, 128, 2 * n)
    return np.ascontiguousarray(words), np.ascontiguousarray(byte.astype(np.uint8).reshape(k // 512, 16, n))


def unpack_weight(words, scales, fmt):
    g, _, n = scales.shape
    words = np.ascontiguousarray(words).reshape(g, 128, n, -1)
    if fmt == "e4m3":
        vals = words.view(ml_dtypes.float8_e4m3fn).astype(np.float64)
    else:
        nib = np.empty((g, 128, n, 4), np.uint8)
        nib[..., 0::2] = words & 0xF
        nib[..., 1::2] = words >> 4
        vals = E2M1[nib]
    vals = vals * np.repeat(np.exp2(scales.astype(np.float64) - 127.0), 8, axis=1)[..., None]
    return vals.transpose(0, 1, 3, 2).reshape(g * 512, n)


def gelu(v):
    return 0.5 * v * (1.0 + np.tanh(np.sqrt(2.0 / np.pi) * (v + 0.044715 * v**3)))


T, S, P, T2, K, K2, H, N = 2048, 1024, 512, 2048, 512, 1024, 1024, 512


def setup_inputs():
    n = np.random.standard_normal
    s, s2, u = mx_kscale(K)[:, None], mx_kscale(K2)[:, None], mx_kscale(H)[:, None]
    tab_words, tab_scales = pack_weight(n((K, T)) * s, "e4m3")
    tab2_words, tab2_scales = pack_weight(n((K2, T)) * s2, "e4m3")
    w1 = (1.4 * n((K, H)) / np.sqrt(K) / s).astype(np.float32)
    w2_words, w2_scales = pack_weight(n((K2, H)) / np.sqrt(K2) / s2 * u.T, "e2m1")
    w3 = (n((K2, H)) / np.sqrt(K2) / s2 * u.T).astype(np.float32)
    gain = (u[:, 0] * np.exp(0.4 * n(H))).astype(np.float32)
    w4 = (1.3 * n((H, N)) / np.sqrt(H) / u).astype(np.float32)
    w5_words, w5_scales = pack_weight(n((H, N)) / np.sqrt(H) / u, "e2m1")
    perm = np.random.permutation(T2)
    return {"tab_words": tab_words, "tab_scales": tab_scales, "tab2_words": tab2_words, "tab2_scales": tab2_scales,
            "offs": striped(np.random.permutation(T)[:S]), "offs2": striped(np.random.permutation(T)[:P]),
            "pos1": striped(np.random.permutation(S)[:P]), "offs3": striped(perm[:S]), "offs4": striped(perm[S:S + P]),
            "w1": w1, "w2_words": w2_words, "w2_scales": w2_scales, "w3": w3, "gain": gain,
            "w4": w4, "w5_words": w5_words, "w5_scales": w5_scales,
            "base1": (0.8 * n((N, S))).astype(np.float32), "page1": n((N, T2)).astype(np.float32),
            "wg1": np.exp(0.3 * n((128, S))).astype(np.float32), "wg2": np.exp(0.3 * n((128, P))).astype(np.float32)}


def reference(tab_words, tab_scales, tab2_words, tab2_scales, offs, offs2, pos1, offs3, offs4, w1, w2_words, w2_scales, w3,
              gain, w4, w5_words, w5_scales, base1, page1, wg1, wg2):
    v = unpack_weight(tab_words, tab_scales, "e4m3")[:, unstriped(offs)]
    v2 = unpack_weight(tab2_words, tab2_scales, "e4m3")[:, unstriped(offs2)]
    h1 = mxq(f64(w1), 0, "e4m3").T @ v
    z1 = f64(gain)[:, None] * np.tanh(h1)
    ha = unpack_weight(w2_words, w2_scales, "e2m1").T @ v2
    hb = mxq(f64(w3), 0, "e4m3").T @ v2
    h2 = np.maximum(ha, hb)
    z2 = h2 * h1[:, unstriped(pos1)]
    y1 = (mxq(f64(w4), 0, "e4m3").T @ mxq(z1, 0, "e4m3")) + f64(base1)
    y2 = unpack_weight(w5_words, w5_scales, "e2m1").T @ mxq(z2, 0, "e4m3")
    out = f64(page1).copy()
    out[:, unstriped(offs3)] = np.tile(f64(wg1), (N // 128, 1)) * y1
    out[:, unstriped(offs4)] = np.tile(f64(wg2), (N // 128, 1)) * y2
    return out

@@ -1,0 +1,300 @@
+from contextlib import ExitStack
+
+import concourse.mybir as mybir
+
+T, S, NP, T2, K, K2, H, N = 2048, 1024, 512, 2048, 512, 1024, 1024, 512
+FLOPS = 2 * (K * H * S + 2 * K2 * H * NP + H * N * S + H * N * NP)
+
+F32 = mybir.dt.float32
+BF16 = mybir.dt.bfloat16
+I32 = mybir.dt.int32
+U32 = mybir.dt.uint32
+U16 = mybir.dt.uint16
+U8 = mybir.dt.uint8
+FP8X4 = mybir.dt.float8_e4m3fn_x4
+FP4X4 = mybir.dt.float4_e2m1fn_x4
+ALU = mybir.AluOpType
+ACT = mybir.ActivationFunctionType
+
+P = 128
+W = 512
+PIECES = ((0, 512), (512, 512))
+
+
+def tile_list_buyer_limit_features_kernel(
+    tc, tab_words, tab_scales, tab2_words, tab2_scales, offs, offs2, pos1, offs3, offs4, w1, w2_words, w2_scales, w3,
+    gain, w4, w5_words, w5_scales, base1, page1, wg1, wg2, out
+):
+    nc = tc.nc
+    with ExitStack() as ctx:
+        lists = ctx.enter_context(tc.tile_pool(name="lists", bufs=1))
+        keep = ctx.enter_context(tc.tile_pool(name="keep", bufs=1))
+        ring = ctx.enter_context(tc.tile_pool(name="ring", bufs=1))
+        psum = ctx.enter_context(tc.psum_pool(name="psum", bufs=1))
+
+        def held(shape, dtype, name, tag=None):
+            return keep.tile(shape, dtype, name=name, tag=tag or name, align_bytes=64)
+
+        def load_list(src, name):
+            t = lists.tile([P, src.shape[1]], U16, name=name)
+            nc.sync.dma_start(t[:], src)
+            return t
+
+        def raw_tile(shape, dtype, name):
+            return ring.tile(shape, dtype, name=name, tag="raw", bufs=6, align_bytes=64)
+
+        def stage_tile(name, cols=W):
+            return ring.tile([P, 4 * cols], BF16, name=name, tag="stage", bufs=4, align_bytes=64)
+
+        def planes_tile(name, cols=W):
+            return ring.tile([P, 4, cols], F32, name=name, tag="planes", bufs=2, align_bytes=64)
+
+        def bank(name, tag):
+            return psum.tile([P, W], F32, name=name, tag=tag, bufs=2)
+
+        def load_words(src, name):
+            t = raw_tile([P, T], I32, name)
+            nc.sync.dma_start(t[:], src.rearrange("p t i -> p (t i)").bitcast(I32))
+            return t
+
+        def load_rows(src, name):
+            t = raw_tile([P, 4, W], F32, name)
+            nc.sync.dma_start(t[:], src.rearrange("(p i) c -> p i c", i=4))
+            return t
+
+        def zeroed_bytes(cols, name):
+            t = held([P, cols], U8, name)
+            nc.vector.memset(t[:].bitcast(I32), 0)
+            return t
+
+        def load_scale_rows(tile, src):
+            for q in range(4):
+                nc.gpsimd.dma_start(
+                    tile[32 * q : 32 * q + 4, :].bitcast(I32).rearrange("p (a c) -> p a c", a=2),
+                    src[:, 4 * q : 4 * q + 4, :].bitcast(I32).rearrange("a r c -> r a c"),
+                )
+
+        def round_dealt(raw, name):
+            st = stage_tile(name)
+            nc.scalar.copy(
+                st[:].rearrange("p (u v m i) -> p u m i v", u=2, v=2, i=4),
+                raw[:].rearrange("p i (m u v) -> p u m i v", u=2, v=2),
+            )
+            return st
+
+        def woven_out(st):
+            return st[:].rearrange("p (c e i) -> p c i e", e=4, i=4)
+
+        def woven_in(planes):
+            return planes[:].rearrange("p i (c e) -> p c i e", e=4)
+
+        def quantise(st, name, tag=None):
+            cols = st.shape[1] // 4
+            codes = held([P, cols], U32, name + "_codes", tag and tag + "_codes")
+            scales = held([P, cols], U8, name + "_scales", tag and tag + "_scales")
+            nc.vector.quantize_mx(out=codes[:].bitcast(FP8X4), scales=scales[:], in_=st[:])
+            return codes, scales
+
+        def mx(acc, lhs, lhs_scale, rhs, rhs_scale, first, last):
+            nc.tensor.matmul_mx(out=acc, lhsT=lhs, lhsT_scale=lhs_scale, rhs=rhs, rhs_scale=rhs_scale, start=first, stop=last)
+
+        offs_sb = load_list(offs, "offs_sb")
+        tab_s = held([P, T], U8, "tab_s")
+        for q in range(4):
+            rows = tab_scales[0, 4 * q : 4 * q + 4, :].bitcast(I32)
+            nc.sync.dma_start(tab_s[32 * q : 32 * q + 32, :].bitcast(I32), rows.unsqueeze(0).to_broadcast([8, 4, T // 4]))
+        tab_w = load_words(tab_words[0], "tab_w")
+        w1_raw = [load_rows(w1[:, b * W : (b + 1) * W], f"w1_raw{b}") for b in range(2)]
+        tab2_s = zeroed_bytes(T, "tab2_s")
+        w2_sraw = zeroed_bytes(2 * H, "w2_sraw")
+        w5_s = zeroed_bytes(2 * N, "w5_s")
+        for q in range(4):
+            nc.gpsimd.dma_start(tab2_s[32 * q : 32 * q + 8, :].bitcast(I32), tab2_scales[:, 4 * q : 4 * q + 4, :].bitcast(I32))
+        load_scale_rows(w2_sraw, w2_scales)
+        load_scale_rows(w5_s, w5_scales)
+        offs2_sb = load_list(offs2, "offs2_sb")
+        tab2_w = [load_words(tab2_words[a], f"tab2_w{a}") for a in range(2)]
+        gain_sb = held([P, 2, 4], F32, "gain_sb")
+        nc.sync.dma_start(gain_sb[:], gain.rearrange("(b p t) -> p b t", b=2, t=4))
+        w4_raw = [load_rows(w4[a * W : (a + 1) * W, :], f"w4_raw{a}") for a in range(2)]
+        offs3_sb = load_list(offs3, "offs3_sb")
+        wg1_sb = [held([P, W], F32, f"wg1_sb{h}") for h in range(2)]
+        base_sb = {}
+        page = [held([P, T2], F32, f"page{c}") for c in range(4)]
+
+        def load_base(c, h):
+            base_sb[c, h] = held([P, W], F32, f"base{c}_{h}")
+            nc.sync.dma_start(base_sb[c, h][:], base1[c * P : (c + 1) * P, h * W : (h + 1) * W])
+
+        nc.sync.dma_start(wg1_sb[0][:], wg1[:, 0:W])
+        for c in range(4):
+            load_base(c, 0)
+            nc.sync.dma_start(page[c][:], page1[c * P : (c + 1) * P, :])
+
+        v_w, v_s = [], []
+        for h in range(2):
+            v_s.append(held([P, W], U8, f"v_s{h}"))
+            nc.vector.tensor_copy(v_s[h][:], tab_s[:].indirect(offs_sb[:, h * 32 : (h + 1) * 32]))
+        for h in range(2):
+            v_w.append(held([P, W], U32, f"v_w{h}"))
+            nc.vector.tensor_copy(v_w[h][:], tab_w[:].bitcast(U32).indirect(offs_sb[:, h * 32 : (h + 1) * 32]))
+        w1_q = [quantise(round_dealt(w1_raw[b], f"w1_bf{b}"), f"w1_{b}", f"qa{b}") for b in range(2)]
+
+        h1 = [held([P, S], F32, f"h1_{r}") for r in range(8)]
+        z1_q = {}
+
+        def first_product(acc, k, b, t):
+            j0, n = PIECES[k]
+            h, j = divmod(j0, W)
+            cols = slice(t * P, (t + 1) * P)
+            mx(acc, w1_q[b][0][:, cols].bitcast(FP8X4), w1_q[b][1][:, cols],
+               v_w[h][:, j : j + n].bitcast(FP8X4), v_s[h][:, j : j + n], True, True)
+
+        def gain_on_vector(k, b, th):
+            st = stage_tile(f"z1_bf{k}{b}")
+            g = gain_sb[:, b, :].unsqueeze(1).unsqueeze(3).to_broadcast([P, W // 4, 4, 4])
+            nc.vector.tensor_tensor(woven_out(st), woven_in(th), g, ALU.mult)
+            z1_q[k, b] = quantise(st, f"z1_{k}{b}")
+
+        def gain_on_scalar(k, b, th):
+            n = PIECES[k][1]
+            flat = stage_tile(f"z1_flat{k}{b}", n)
+            for t in range(4):
+                nc.scalar.activation(flat[:, t * n : (t + 1) * n], th[:, t, :], ACT.Copy, scale=gain_sb[:, b, t : t + 1])
+            st = stage_tile(f"z1_bf{k}{b}", n)
+            nc.scalar.copy(woven_out(st), flat[:].rearrange("p (i c e) -> p c i e", i=4, e=4))
+            z1_q[k, b] = quantise(st, f"z1_{k}{b}")
+
+        def later_piece(k):
+            j0, n = PIECES[k]
+            for b in range(2):
+                th = planes_tile(f"th{k}{b}", n)
+                for t in range(4):
+                    acc = bank(f"h_acc{k}{b}{t}", "h")
+                    first_product(acc[:], k, b, t)
+                    nc.scalar.activation(th[:, t, :], acc[:], ACT.Tanh)
+                    nc.scalar.copy(h1[4 * b + t][:, j0 : j0 + n], acc[:])
+                gain_on_scalar(k, b, th)
+
+        def buyers_out(k, c, y=None):
+            j0, n = PIECES[k]
+            h, j = divmod(j0, W)
+            acc = bank(f"y1_acc{k}{c}", "y")
+            cols = slice(c * P, (c + 1) * P)
+            for a in (1, 0):
+                mx(acc[:, 0:n], w4_q[a][0][:, cols].bitcast(FP8X4), w4_q[a][1][:, cols],
+                   z1_q[k, a][0][:].bitcast(FP8X4), z1_q[k, a][1][:], a == 1, a == 0)
+            base = base_sb[c, h][:, j : j + n]
+            if y is None:
+                y = base
+            nc.vector.tensor_tensor(y, acc[:, 0:n], base, ALU.add)
+            part = offs3_sb[:, j0 // 16 : (j0 + n) // 16]
+            nc.vector.tensor_tensor(page[c][:].indirect(part), y, wg1_sb[h][:, j : j + n], ALU.mult)
+
+        accs = []
+        for b in range(2):
+            th = planes_tile(f"th0{b}")
+            for t in range(4):
+                accs.append(bank(f"h_acc0{b}{t}", ("y", "h", "ha", "hb")[2 * b + t // 2]))
+                first_product(accs[-1][:], 0, b, t)
+                nc.scalar.activation(th[:, t, :], accs[-1][:], ACT.Tanh)
+            gain_on_vector(0, b, th)
+        for r in range(8):
+            nc.scalar.copy(h1[r][:, 0:W], accs[r][:])
+
+        w4_q = []
+        for a in range(2):
+            st = stage_tile(f"w4_bf{a}")
+            nc.vector.tensor_copy(woven_out(st), woven_in(w4_raw[a]))
+            w4_q.append(quantise(st, f"w4_{a}"))
+
+        v2_s0 = held([P, W], U8, "v2_s0")
+        nc.vector.tensor_copy(v2_s0[:], tab2_s[:].indirect(offs2_sb[:]))
+        v2_w = []
+        for a in range(2):
+            v2_w.append(held([P, W], U32, f"v2_w{a}"))
+            nc.vector.tensor_copy(v2_w[a][:], tab2_w[a][:].bitcast(U32).indirect(offs2_sb[:]))
+        v2_s1 = zeroed_bytes(W, "v2_s1")
+        nc.gpsimd.dma_start(v2_s1[0 : P - 4, :].bitcast(I32), v2_s0[4:P, :].bitcast(I32))
+        v2_s = [v2_s0, v2_s1]
+
+        nc.sync.dma_start(wg1_sb[1][:], wg1[:, W:S])
+        for c in range(4):
+            load_base(c, 1)
+        w3_raw = {}
+        for a in range(2):
+            w3_raw[a, 0] = load_rows(w3[a * W : (a + 1) * W, 0:W], f"w3_raw{a}0")
+        w2_raw = held([P, 4 * H], U8, "w2_raw")
+        nc.sync.dma_start(w2_raw[:].bitcast(I32).rearrange("p (a c) -> p a c", a=2), w2_words.bitcast(I32).rearrange("a p c -> p a c"))
+        for a in range(2):
+            w3_raw[a, 1] = load_rows(w3[a * W : (a + 1) * W, W:H], f"w3_raw{a}1")
+        pos1_sb = load_list(pos1, "pos1_sb")
+        offs4_sb = load_list(offs4, "offs4_sb")
+        w5_w = held([P, 4 * N], U8, "w5_w")
+        nc.sync.dma_start(w5_w[:].bitcast(I32).rearrange("p (a c) -> p a c", a=2), w5_words.bitcast(I32).rearrange("a p c -> p a c"))
+        wg2_sb = held([P, NP], F32, "wg2_sb")
+        nc.sync.dma_start(wg2_sb[:], wg2)
+
+        for c in range(4):
+            buyers_out(0, c)
+        later_piece(1)
+        for c in range(2):
+            buyers_out(1, c)
+
+        w2_w = held([P, 4 * H], U8, "w2_w")
+        w2_s = held([P, 2 * H], U8, "w2_s")
+        nc.vector.tensor_copy(
+            w2_s[:].rearrange("p (g t m) -> p g t m", g=4, t=4),
+            w2_sraw[:].rearrange("p (g m t) -> p g t m", g=4, t=4),
+        )
+
+        w3_q = {}
+        z2_q = []
+
+        def quantise_w3(b):
+            for a in range(2):
+                w3_q[a, b] = quantise(round_dealt(w3_raw[a, b], f"w3_bf{a}{b}"), f"w3_{a}{b}")
+
+        def holders_stage(b):
+            z2 = planes_tile(f"z2_{b}")
+            for t in range(4):
+                ha = bank(f"ha{b}{t}", "ha")
+                hb = bank(f"hb{b}{t}", "hb")
+                cols = slice(t * P, (t + 1) * P)
+                for a in range(2):
+                    c0 = a * H + b * W + t * P
+                    mx(ha[:], w2_w[:, 2 * c0 : 2 * c0 + 2 * P].bitcast(FP4X4), w2_s[:, c0 : c0 + P],
+                       v2_w[a][:].bitcast(FP8X4), v2_s[a][:], a == 0, a == 1)
+                for a in (1, 0):
+                    mx(hb[:], w3_q[a, b][0][:, cols].bitcast(FP8X4), w3_q[a, b][1][:, cols],
+                       v2_w[a][:].bitcast(FP8X4), v2_s[a][:], a == 1, a == 0)
+                h2 = ring.tile([P, W], F32, name=f"h2_{b}{t}", tag="h2", bufs=3, align_bytes=64)
+                nc.scalar.copy(h2[:], ha[:])
+                nc.vector.tensor_tensor(h2[:], hb[:], h2[:], ALU.max)
+                nc.vector.tensor_tensor(z2[:, t, :], h1[4 * b + t][:].indirect(pos1_sb[:]), h2[:], ALU.mult)
+            st = stage_tile(f"z2_bf{b}")
+            nc.scalar.copy(woven_out(st), woven_in(z2))
+            z2_q.append(quantise(st, f"z2_{b}", f"qa{b}"))
+            return h2, z2
+
+        quantise_w3(0)
+        nc.scalar.copy(
+            w2_w[:].bitcast(U16).rearrange("p (g t m) -> p g t m", g=4, t=4),
+            w2_raw[:].bitcast(U16).rearrange("p (g m t) -> p g t m", g=4, t=4),
+        )
+        holders_stage(0)
+        quantise_w3(1)
+        h2, z2 = holders_stage(1)
+        buyers_out(1, 2, h2[:])
+        buyers_out(1, 3, z2[:, 0, :])
+
+        for c in range(4):
+            acc = bank(f"y2_acc{c}", "y")
+            for a in (1, 0):
+                c0 = a * N + c * P
+                mx(acc[:], w5_w[:, 2 * c0 : 2 * c0 + 2 * P].bitcast(FP4X4), w5_s[:, c0 : c0 + P],
+                   z2_q[a][0][:].bitcast(FP8X4), z2_q[a][1][:], a == 1, a == 0)
+            y2 = ring.tile([P, W], F32, name=f"y2_{c}", tag="h2", bufs=3, align_bytes=64)
+            nc.scalar.copy(y2[:], acc[:])
+            nc.vector.tensor_tensor(page[c][:].indirect(offs4_sb[:]), y2[:], wg2_sb[:], ALU.mult)
+            nc.sync.dma_start(out[c * P : (c + 1) * P, :], page[c][:])

@@ -69,14 +69,14 @@ def tile_list_buyer_limit_features_kernel(
 
         def load_scale_rows(tile, src):
             for q in range(4):
-                nc.gpsimd.dma_start(
+                nc.sync.dma_start(
                     tile[32 * q : 32 * q + 4, :].bitcast(I32).rearrange("p (a c) -> p a c", a=2),
                     src[:, 4 * q : 4 * q + 4, :].bitcast(I32).rearrange("a r c -> r a c"),
                 )
 
-        def round_dealt(raw, name):
+        def round_dealt(raw, name, copy=nc.scalar.copy):
             st = stage_tile(name)
-            nc.scalar.copy(
+            copy(
                 st[:].rearrange("p (u v m i) -> p u m i v", u=2, v=2, i=4),
                 raw[:].rearrange("p i (m u v) -> p u m i v", u=2, v=2),
             )
@@ -90,8 +90,8 @@ def tile_list_buyer_limit_features_kernel(
 
         def quantise(st, name, tag=None):
             cols = st.shape[1] // 4
-            codes = held([P, cols], U32, name + "_codes", tag and tag + "_codes")
-            scales = held([P, cols], U8, name + "_scales", tag and tag + "_scales")
+            codes = held([P, cols], U32, name + "_codes", tag)
+            scales = held([P, cols], U8, name + "_scales")
             nc.vector.quantize_mx(out=codes[:].bitcast(FP8X4), scales=scales[:], in_=st[:])
             return codes, scales
 
@@ -104,16 +104,16 @@ def tile_list_buyer_limit_features_kernel(
             rows = tab_scales[0, 4 * q : 4 * q + 4, :].bitcast(I32)
             nc.sync.dma_start(tab_s[32 * q : 32 * q + 32, :].bitcast(I32), rows.unsqueeze(0).to_broadcast([8, 4, T // 4]))
         tab_w = load_words(tab_words[0], "tab_w")
-        w1_raw = [load_rows(w1[:, b * W : (b + 1) * W], f"w1_raw{b}") for b in range(2)]
+        offs2_sb = load_list(offs2, "offs2_sb")
+        w1_raw = [load_rows(w1[:, 0:W], "w1_raw0")]
         tab2_s = zeroed_bytes(T, "tab2_s")
         w2_sraw = zeroed_bytes(2 * H, "w2_sraw")
         w5_s = zeroed_bytes(2 * N, "w5_s")
         for q in range(4):
-            nc.gpsimd.dma_start(tab2_s[32 * q : 32 * q + 8, :].bitcast(I32), tab2_scales[:, 4 * q : 4 * q + 4, :].bitcast(I32))
+            nc.sync.dma_start(tab2_s[32 * q : 32 * q + 8, :].bitcast(I32), tab2_scales[:, 4 * q : 4 * q + 4, :].bitcast(I32))
+        w2_raw = [held([P, 2 * H], U8, f"w2_raw{a}") for a in range(2)]
+        w1_raw.append(load_rows(w1[:, W:H], "w1_raw1"))
         load_scale_rows(w2_sraw, w2_scales)
-        load_scale_rows(w5_s, w5_scales)
-        offs2_sb = load_list(offs2, "offs2_sb")
-        tab2_w = [load_words(tab2_words[a], f"tab2_w{a}") for a in range(2)]
         gain_sb = held([P, 2, 4], F32, "gain_sb")
         nc.sync.dma_start(gain_sb[:], gain.rearrange("(b p t) -> p b t", b=2, t=4))
         w4_raw = [load_rows(w4[a * W : (a + 1) * W, :], f"w4_raw{a}") for a in range(2)]
@@ -126,10 +126,17 @@ def tile_list_buyer_limit_features_kernel(
             base_sb[c, h] = held([P, W], F32, f"base{c}_{h}")
             nc.sync.dma_start(base_sb[c, h][:], base1[c * P : (c + 1) * P, h * W : (h + 1) * W])
 
-        nc.sync.dma_start(wg1_sb[0][:], wg1[:, 0:W])
-        for c in range(4):
-            load_base(c, 0)
+        def load_page(c):
             nc.sync.dma_start(page[c][:], page1[c * P : (c + 1) * P, :])
+
+        tab2_w = [load_words(tab2_words[0], "tab2_w0")]
+        nc.sync.dma_start(wg1_sb[0][:], wg1[:, 0:W])
+        load_base(0, 0)
+        for c in range(3):
+            load_base(c + 1, 0)
+            load_page(c)
+        tab2_w.append(load_words(tab2_words[1], "tab2_w1"))
+        load_page(3)
 
         v_w, v_s = [], []
         for h in range(2):
@@ -138,7 +145,7 @@ def tile_list_buyer_limit_features_kernel(
         for h in range(2):
             v_w.append(held([P, W], U32, f"v_w{h}"))
             nc.vector.tensor_copy(v_w[h][:], tab_w[:].bitcast(U32).indirect(offs_sb[:, h * 32 : (h + 1) * 32]))
-        w1_q = [quantise(round_dealt(w1_raw[b], f"w1_bf{b}"), f"w1_{b}", f"qa{b}") for b in range(2)]
+        w1_q = [quantise(round_dealt(w1_raw[b], f"w1_bf{b}", (nc.scalar.copy, nc.vector.tensor_copy)[b]), f"w1_{b}", f"qa{b}") for b in range(2)]
 
         h1 = [held([P, S], F32, f"h1_{r}") for r in range(8)]
         z1_q = {}
@@ -163,10 +170,11 @@ def tile_list_buyer_limit_features_kernel(
                 nc.scalar.activation(flat[:, t * n : (t + 1) * n], th[:, t, :], ACT.Copy, scale=gain_sb[:, b, t : t + 1])
             st = stage_tile(f"z1_bf{k}{b}", n)
             nc.scalar.copy(woven_out(st), flat[:].rearrange("p (i c e) -> p c i e", i=4, e=4))
-            z1_q[k, b] = quantise(st, f"z1_{k}{b}")
+            return st
 
         def later_piece(k):
             j0, n = PIECES[k]
+            done = []
             for b in range(2):
                 th = planes_tile(f"th{k}{b}", n)
                 for t in range(4):
@@ -174,7 +182,8 @@ def tile_list_buyer_limit_features_kernel(
                     first_product(acc[:], k, b, t)
                     nc.scalar.activation(th[:, t, :], acc[:], ACT.Tanh)
                     nc.scalar.copy(h1[4 * b + t][:, j0 : j0 + n], acc[:])
-                gain_on_scalar(k, b, th)
+                done.append(gain_on_scalar(k, b, th))
+            return done
 
         def buyers_out(k, c, y=None):
             j0, n = PIECES[k]
@@ -199,7 +208,7 @@ def tile_list_buyer_limit_features_kernel(
                 first_product(accs[-1][:], 0, b, t)
                 nc.scalar.activation(th[:, t, :], accs[-1][:], ACT.Tanh)
             gain_on_vector(0, b, th)
-        for r in range(8):
+        for r in range(2):
             nc.scalar.copy(h1[r][:, 0:W], accs[r][:])
 
         w4_q = []
@@ -207,6 +216,8 @@ def tile_list_buyer_limit_features_kernel(
             st = stage_tile(f"w4_bf{a}")
             nc.vector.tensor_copy(woven_out(st), woven_in(w4_raw[a]))
             w4_q.append(quantise(st, f"w4_{a}"))
+        for r in range(2, 8):
+            nc.scalar.copy(h1[r][:, 0:W], accs[r][:])
 
         v2_s0 = held([P, W], U8, "v2_s0")
         nc.vector.tensor_copy(v2_s0[:], tab2_s[:].indirect(offs2_sb[:]))
@@ -219,16 +230,23 @@ def tile_list_buyer_limit_features_kernel(
         v2_s = [v2_s0, v2_s1]
 
         nc.sync.dma_start(wg1_sb[1][:], wg1[:, W:S])
-        for c in range(4):
-            load_base(c, 1)
         w3_raw = {}
+
+        def load_w3(a, b):
+            w3_raw[a, b] = load_rows(w3[a * W : (a + 1) * W, b * W : (b + 1) * W], f"w3_raw{a}{b}")
+
+        load_w3(0, 0)
+        load_w3(1, 0)
+        load_base(0, 1)
+        load_base(1, 1)
+        load_w3(0, 1)
+        load_w3(1, 1)
         for a in range(2):
-            w3_raw[a, 0] = load_rows(w3[a * W : (a + 1) * W, 0:W], f"w3_raw{a}0")
-        w2_raw = held([P, 4 * H], U8, "w2_raw")
-        nc.sync.dma_start(w2_raw[:].bitcast(I32).rearrange("p (a c) -> p a c", a=2), w2_words.bitcast(I32).rearrange("a p c -> p a c"))
-        for a in range(2):
-            w3_raw[a, 1] = load_rows(w3[a * W : (a + 1) * W, W:H], f"w3_raw{a}1")
+            nc.sync.dma_start(w2_raw[a][:].bitcast(I32), w2_words[a].bitcast(I32))
         pos1_sb = load_list(pos1, "pos1_sb")
+        load_base(2, 1)
+        load_base(3, 1)
+        load_scale_rows(w5_s, w5_scales)
         offs4_sb = load_list(offs4, "offs4_sb")
         w5_w = held([P, 4 * N], U8, "w5_w")
         nc.sync.dma_start(w5_w[:].bitcast(I32).rearrange("p (a c) -> p a c", a=2), w5_words.bitcast(I32).rearrange("a p c -> p a c"))
@@ -237,11 +255,12 @@ def tile_list_buyer_limit_features_kernel(
 
         for c in range(4):
             buyers_out(0, c)
-        later_piece(1)
+        for b, st in enumerate(later_piece(1)):
+            z1_q[1, b] = quantise(st, f"z1_1{b}", f"base{2 * b + 1}_0")
         for c in range(2):
             buyers_out(1, c)
 
-        w2_w = held([P, 4 * H], U8, "w2_w")
+        w2_w = [held([P, 2 * H], U8, f"w2_w{a}") for a in range(2)]
         w2_s = held([P, 2 * H], U8, "w2_s")
         nc.vector.tensor_copy(
             w2_s[:].rearrange("p (g t m) -> p g t m", g=4, t=4),
@@ -261,14 +280,14 @@ def tile_list_buyer_limit_features_kernel(
                 ha = bank(f"ha{b}{t}", "ha")
                 hb = bank(f"hb{b}{t}", "hb")
                 cols = slice(t * P, (t + 1) * P)
-                for a in range(2):
-                    c0 = a * H + b * W + t * P
-                    mx(ha[:], w2_w[:, 2 * c0 : 2 * c0 + 2 * P].bitcast(FP4X4), w2_s[:, c0 : c0 + P],
-                       v2_w[a][:].bitcast(FP8X4), v2_s[a][:], a == 0, a == 1)
+                for a in (1, 0):
+                    c0 = b * W + t * P
+                    mx(ha[:], w2_w[a][:, 2 * c0 : 2 * c0 + 2 * P].bitcast(FP4X4), w2_s[:, a * H + c0 : a * H + c0 + P],
+                       v2_w[a][:].bitcast(FP8X4), v2_s[a][:], a == 1, a == 0)
                 for a in (1, 0):
                     mx(hb[:], w3_q[a, b][0][:, cols].bitcast(FP8X4), w3_q[a, b][1][:, cols],
                        v2_w[a][:].bitcast(FP8X4), v2_s[a][:], a == 1, a == 0)
-                h2 = ring.tile([P, W], F32, name=f"h2_{b}{t}", tag="h2", bufs=3, align_bytes=64)
+                h2 = ring.tile([P, W], F32, name=f"h2_{b}{t}", tag="h2", bufs=4, align_bytes=64)
                 nc.scalar.copy(h2[:], ha[:])
                 nc.vector.tensor_tensor(h2[:], hb[:], h2[:], ALU.max)
                 nc.vector.tensor_tensor(z2[:, t, :], h1[4 * b + t][:].indirect(pos1_sb[:]), h2[:], ALU.mult)
@@ -278,12 +297,13 @@ def tile_list_buyer_limit_features_kernel(
             return h2, z2
 
         quantise_w3(0)
-        nc.scalar.copy(
-            w2_w[:].bitcast(U16).rearrange("p (g t m) -> p g t m", g=4, t=4),
-            w2_raw[:].bitcast(U16).rearrange("p (g m t) -> p g t m", g=4, t=4),
-        )
-        holders_stage(0)
         quantise_w3(1)
+        for a in range(2):
+            nc.scalar.copy(
+                w2_w[a][:].bitcast(U16).rearrange("p (b t m) -> p b t m", b=2, t=4),
+                w2_raw[a][:].bitcast(U16).rearrange("p (b m t) -> p b t m", b=2, t=4),
+            )
+        holders_stage(0)
         h2, z2 = holders_stage(1)
         buyers_out(1, 2, h2[:])
         buyers_out(1, 3, z2[:, 0, :])
@@ -294,7 +314,7 @@ def tile_list_buyer_limit_features_kernel(
                 c0 = a * N + c * P
                 mx(acc[:], w5_w[:, 2 * c0 : 2 * c0 + 2 * P].bitcast(FP4X4), w5_s[:, c0 : c0 + P],
                    z2_q[a][0][:].bitcast(FP8X4), z2_q[a][1][:], a == 1, a == 0)
-            y2 = ring.tile([P, W], F32, name=f"y2_{c}", tag="h2", bufs=3, align_bytes=64)
+            y2 = ring.tile([P, W], F32, name=f"y2_{c}", tag="h2", bufs=4, align_bytes=64)
             nc.scalar.copy(y2[:], acc[:])
             nc.vector.tensor_tensor(page[c][:].indirect(offs4_sb[:]), y2[:], wg2_sb[:], ALU.mult)
             nc.sync.dma_start(out[c * P : (c + 1) * P, :], page[c][:])

@@ -82,11 +82,11 @@ def tile_list_buyer_limit_features_kernel(
             )
             return st
 
-        def woven_out(st):
-            return st[:].rearrange("p (c e i) -> p c i e", e=4, i=4)
+        def woven_out(st, e=2):
+            return st[:].rearrange("p (c e i) -> p c i e", e=e, i=4)
 
         def woven_in(planes):
-            return planes[:].rearrange("p i (c e) -> p c i e", e=4)
+            return planes[:].rearrange("p i (c e) -> p c i e", e=2)
 
         def quantise(st, name, tag=None):
             cols = st.shape[1] // 4
@@ -159,7 +159,7 @@ def tile_list_buyer_limit_features_kernel(
 
         def gain_on_vector(k, b, th):
             st = stage_tile(f"z1_bf{k}{b}")
-            g = gain_sb[:, b, :].unsqueeze(1).unsqueeze(3).to_broadcast([P, W // 4, 4, 4])
+            g = gain_sb[:, b, :].unsqueeze(1).unsqueeze(3).to_broadcast([P, W // 2, 4, 2])
             nc.vector.tensor_tensor(woven_out(st), woven_in(th), g, ALU.mult)
             z1_q[k, b] = quantise(st, f"z1_{k}{b}")
 
@@ -169,7 +169,7 @@ def tile_list_buyer_limit_features_kernel(
             for t in range(4):
                 nc.scalar.activation(flat[:, t * n : (t + 1) * n], th[:, t, :], ACT.Copy, scale=gain_sb[:, b, t : t + 1])
             st = stage_tile(f"z1_bf{k}{b}", n)
-            nc.scalar.copy(woven_out(st), flat[:].rearrange("p (i c e) -> p c i e", i=4, e=4))
+            nc.scalar.copy(woven_out(st, 4), flat[:].rearrange("p (i c e) -> p c i e", i=4, e=4))
             return st
 
         def later_piece(k):

@@ -18,7 +18,6 @@ ACT = mybir.ActivationFunctionType
 
 P = 128
 W = 512
-PIECES = ((0, 512), (512, 512))
 
 
 def tile_list_buyer_limit_features_kernel(
@@ -35,100 +34,117 @@ def tile_list_buyer_limit_features_kernel(
         def held(shape, dtype, name, tag=None):
             return keep.tile(shape, dtype, name=name, tag=tag or name, align_bytes=64)
 
-        def load_list(src, name):
-            t = lists.tile([P, src.shape[1]], U16, name=name)
-            nc.sync.dma_start(t[:], src)
-            return t
-
         def raw_tile(shape, dtype, name):
             return ring.tile(shape, dtype, name=name, tag="raw", bufs=6, align_bytes=64)
 
-        def stage_tile(name, cols=W):
-            return ring.tile([P, 4 * cols], BF16, name=name, tag="stage", bufs=4, align_bytes=64)
+        def stage_tile(name, operands):
+            return ring.tile([P, operands * 4 * W], BF16, name=name, tag="stage", bufs=3, align_bytes=64)
 
-        def planes_tile(name, cols=W):
-            return ring.tile([P, 4, cols], F32, name=name, tag="planes", bufs=2, align_bytes=64)
+        def planes_tile(name):
+            return ring.tile([P, 4, W], F32, name=name, tag="planes", bufs=2, align_bytes=64)
+
+        def row_tile(name):
+            return ring.tile([P, W], F32, name=name, tag="row", bufs=4, align_bytes=64)
 
         def bank(name, tag):
             return psum.tile([P, W], F32, name=name, tag=tag, bufs=2)
 
+        def zeroed_bytes(cols, name):
+            tile = held([P, cols], U8, name)
+            nc.vector.memset(tile[:].bitcast(I32), 0)
+            return tile
+
+        def load_list(src, name):
+            tile = lists.tile([P, src.shape[1]], U16, name=name)
+            nc.sync.dma_start(tile[:], src)
+            return tile
+
         def load_words(src, name):
-            t = raw_tile([P, T], I32, name)
-            nc.sync.dma_start(t[:], src.rearrange("p t i -> p (t i)").bitcast(I32))
-            return t
+            tile = raw_tile([P, T], I32, name)
+            nc.sync.dma_start(tile[:], src.rearrange("p t i -> p (t i)").bitcast(I32))
+            return tile
 
         def load_rows(src, name):
-            t = raw_tile([P, 4, W], F32, name)
-            nc.sync.dma_start(t[:], src.rearrange("(p i) c -> p i c", i=4))
-            return t
+            tile = raw_tile([P, 4, W], F32, name)
+            nc.sync.dma_start(tile[:], src.rearrange("(p i) c -> p i c", i=4))
+            return tile
 
-        def zeroed_bytes(cols, name):
-            t = held([P, cols], U8, name)
-            nc.vector.memset(t[:].bitcast(I32), 0)
-            return t
-
-        def load_scale_rows(tile, src):
+        def load_stacked_planes(tile, src):
             for q in range(4):
-                nc.sync.dma_start(
-                    tile[32 * q : 32 * q + 4, :].bitcast(I32).rearrange("p (a c) -> p a c", a=2),
-                    src[:, 4 * q : 4 * q + 4, :].bitcast(I32).rearrange("a r c -> r a c"),
-                )
+                nc.sync.dma_start(tile[32 * q : 32 * q + 8, :].bitcast(I32), src[:, 4 * q : 4 * q + 4, :].bitcast(I32))
 
-        def round_dealt(raw, name, copy=nc.scalar.copy):
-            st = stage_tile(name)
-            copy(
-                st[:].rearrange("p (u v m i) -> p u m i v", u=2, v=2, i=4),
-                raw[:].rearrange("p i (m u v) -> p u m i v", u=2, v=2),
-            )
-            return st
+        def second_plane(stacked, name):
+            tile = zeroed_bytes(stacked.shape[1], name)
+            nc.gpsimd.dma_start(tile[0 : P - 4, :].bitcast(I32), stacked[4:P, :].bitcast(I32))
+            return tile
 
-        def woven_out(st, e=2):
-            return st[:].rearrange("p (c e i) -> p c i e", e=e, i=4)
+        def operand(stage, a):
+            return stage[:, a * 4 * W : (a + 1) * 4 * W]
 
-        def woven_in(planes):
-            return planes[:].rearrange("p i (c e) -> p c i e", e=2)
+        def dealt(bf):
+            return bf.rearrange("p (u v m i) -> p u m i v", u=2, v=2, i=4)
 
-        def quantise(st, name, tag=None):
-            cols = st.shape[1] // 4
-            codes = held([P, cols], U32, name + "_codes", tag)
-            scales = held([P, cols], U8, name + "_scales")
-            nc.vector.quantize_mx(out=codes[:].bitcast(FP8X4), scales=scales[:], in_=st[:])
+        def to_deal(raw):
+            return raw[:].rearrange("p i (m u v) -> p u m i v", u=2, v=2)
+
+        def woven(bf, e):
+            return bf.rearrange("p (c e i) -> p c i e", e=e, i=4)
+
+        def to_weave(planes, e):
+            return planes.rearrange("p i (c e) -> p c i e", e=e)
+
+        def quantise(stage, name, codes_tag=None, scales_tag=None):
+            cols = stage.shape[1] // 4
+            codes = held([P, cols], U32, name + "_codes", codes_tag)
+            scales = held([P, cols], U8, name + "_scales", scales_tag)
+            nc.vector.quantize_mx(out=codes[:].bitcast(FP8X4), scales=scales[:], in_=stage[:])
             return codes, scales
 
-        def mx(acc, lhs, lhs_scale, rhs, rhs_scale, first, last):
-            nc.tensor.matmul_mx(out=acc, lhsT=lhs, lhsT_scale=lhs_scale, rhs=rhs, rhs_scale=rhs_scale, start=first, stop=last)
+        def fp8(quantised, c0, n):
+            return quantised[0][:, c0 : c0 + n].bitcast(FP8X4), quantised[1][:, c0 : c0 + n]
 
-        offs_sb = load_list(offs, "offs_sb")
-        tab_s = held([P, T], U8, "tab_s")
-        for q in range(4):
-            rows = tab_scales[0, 4 * q : 4 * q + 4, :].bitcast(I32)
-            nc.sync.dma_start(tab_s[32 * q : 32 * q + 32, :].bitcast(I32), rows.unsqueeze(0).to_broadcast([8, 4, T // 4]))
-        tab_w = load_words(tab_words[0], "tab_w")
-        offs2_sb = load_list(offs2, "offs2_sb")
-        w1_raw = [load_rows(w1[:, 0:W], "w1_raw0")]
+        def fp4(words, scales, c0, n):
+            return words[:, 2 * c0 : 2 * (c0 + n)].bitcast(FP4X4), scales[:, c0 : c0 + n]
+
+        def product(acc, passes):
+            for n, (lhs, rhs) in enumerate(passes):
+                nc.tensor.matmul_mx(out=acc[:], lhsT=lhs[0], lhsT_scale=lhs[1], rhs=rhs[0], rhs_scale=rhs[1],
+                                    start=n == 0, stop=n == len(passes) - 1)
+
         tab2_s = zeroed_bytes(T, "tab2_s")
-        w2_sraw = zeroed_bytes(2 * H, "w2_sraw")
+        w2_s_raw = zeroed_bytes(H, "w2_s_raw")
         w5_s = zeroed_bytes(2 * N, "w5_s")
-        for q in range(4):
-            nc.sync.dma_start(tab2_s[32 * q : 32 * q + 8, :].bitcast(I32), tab2_scales[:, 4 * q : 4 * q + 4, :].bitcast(I32))
-        w2_raw = [held([P, 2 * H], U8, f"w2_raw{a}") for a in range(2)]
-        w1_raw.append(load_rows(w1[:, W:H], "w1_raw1"))
-        load_scale_rows(w2_sraw, w2_scales)
+        tab_s = held([P, T], U8, "tab_s")
         gain_sb = held([P, 2, 4], F32, "gain_sb")
-        nc.sync.dma_start(gain_sb[:], gain.rearrange("(b p t) -> p b t", b=2, t=4))
-        w4_raw = [load_rows(w4[a * W : (a + 1) * W, :], f"w4_raw{a}") for a in range(2)]
-        offs3_sb = load_list(offs3, "offs3_sb")
         wg1_sb = [held([P, W], F32, f"wg1_sb{h}") for h in range(2)]
-        base_sb = {}
+        wg2_sb = held([P, NP], F32, "wg2_sb")
+        base_sb = {(c, h): held([P, W], F32, f"base{c}_{h}") for c in range(4) for h in range(2)}
         page = [held([P, T2], F32, f"page{c}") for c in range(4)]
+        w2_raw = [held([P, 2 * H], U8, f"w2_raw{a}") for a in range(2)]
+        w5_w = held([P, 4 * N], U8, "w5_w")
 
         def load_base(c, h):
-            base_sb[c, h] = held([P, W], F32, f"base{c}_{h}")
             nc.sync.dma_start(base_sb[c, h][:], base1[c * P : (c + 1) * P, h * W : (h + 1) * W])
 
         def load_page(c):
             nc.sync.dma_start(page[c][:], page1[c * P : (c + 1) * P, :])
 
+        def load_w3(a, b):
+            return load_rows(w3[a * W : (a + 1) * W, b * W : (b + 1) * W], f"w3_raw{a}{b}")
+
+        offs_sb = load_list(offs, "offs_sb")
+        for q in range(4):
+            rows = tab_scales[0, 4 * q : 4 * q + 4, :].bitcast(I32)
+            nc.sync.dma_start(tab_s[32 * q : 32 * q + 32, :].bitcast(I32), rows.unsqueeze(0).to_broadcast([8, 4, T // 4]))
+        tab_w = load_words(tab_words[0], "tab_w")
+        offs2_sb = load_list(offs2, "offs2_sb")
+        w1_raw = [load_rows(w1[:, b * W : (b + 1) * W], f"w1_raw{b}") for b in range(2)]
+        w4_raw = [load_rows(w4[0:W, :], "w4_raw0")]
+        load_stacked_planes(tab2_s, tab2_scales)
+        nc.sync.dma_start(gain_sb[:], gain.rearrange("(b p t) -> p b t", b=2, t=4))
+        w4_raw.append(load_rows(w4[W:H, :], "w4_raw1"))
+        load_stacked_planes(w2_s_raw, w2_scales)
+        offs3_sb = load_list(offs3, "offs3_sb")
         tab2_w = [load_words(tab2_words[0], "tab2_w0")]
         nc.sync.dma_start(wg1_sb[0][:], wg1[:, 0:W])
         load_base(0, 0)
@@ -138,183 +154,143 @@ def tile_list_buyer_limit_features_kernel(
         tab2_w.append(load_words(tab2_words[1], "tab2_w1"))
         load_page(3)
 
-        v_w, v_s = [], []
-        for h in range(2):
-            v_s.append(held([P, W], U8, f"v_s{h}"))
-            nc.vector.tensor_copy(v_s[h][:], tab_s[:].indirect(offs_sb[:, h * 32 : (h + 1) * 32]))
-        for h in range(2):
-            v_w.append(held([P, W], U32, f"v_w{h}"))
-            nc.vector.tensor_copy(v_w[h][:], tab_w[:].bitcast(U32).indirect(offs_sb[:, h * 32 : (h + 1) * 32]))
-        w1_q = [quantise(round_dealt(w1_raw[b], f"w1_bf{b}", (nc.scalar.copy, nc.vector.tensor_copy)[b]), f"w1_{b}", f"qa{b}") for b in range(2)]
+        v_w = held([P, S], U32, "v_w")
+        v_s = held([P, S], U8, "v_s")
+        halves = [(slice(h * W, (h + 1) * W), slice(h * W // 16, (h + 1) * W // 16)) for h in range(2)]
+        for cols, entries in halves:
+            nc.vector.tensor_copy(v_s[:, cols], tab_s[:].indirect(offs_sb[:, entries]))
+        for cols, entries in halves:
+            nc.vector.tensor_copy(v_w[:, cols], tab_w[:].bitcast(U32).indirect(offs_sb[:, entries]))
+
+        w1_bf = [stage_tile(f"w1_bf{b}", 1) for b in range(2)]
+        nc.scalar.copy(dealt(w1_bf[0][:])[:, 0], to_deal(w1_raw[0])[:, 0])
+        nc.vector.tensor_copy(dealt(w1_bf[0][:])[:, 1], to_deal(w1_raw[0])[:, 1])
+        w1_q = [quantise(w1_bf[0], "w1_0")]
+        nc.vector.tensor_copy(dealt(w1_bf[1][:]), to_deal(w1_raw[1]))
+        w1_q.append(quantise(w1_bf[1], "w1_1"))
+
+        v2_s0 = held([P, NP], U8, "v2_s0")
+        nc.vector.tensor_copy(v2_s0[:], tab2_s[:].indirect(offs2_sb[:]))
+        v2_s = [v2_s0, second_plane(v2_s0, "v2_s1")]
 
         h1 = [held([P, S], F32, f"h1_{r}") for r in range(8)]
-        z1_q = {}
 
-        def first_product(acc, k, b, t):
-            j0, n = PIECES[k]
-            h, j = divmod(j0, W)
-            cols = slice(t * P, (t + 1) * P)
-            mx(acc, w1_q[b][0][:, cols].bitcast(FP8X4), w1_q[b][1][:, cols],
-               v_w[h][:, j : j + n].bitcast(FP8X4), v_s[h][:, j : j + n], True, True)
+        def first_product(h, b, t, tag):
+            acc = bank(f"h_acc{h}{b}{t}", tag)
+            product(acc, [(fp8(w1_q[b], t * P, P), fp8((v_w, v_s), h * W, W))])
+            return acc
 
-        def gain_on_vector(k, b, th):
-            st = stage_tile(f"z1_bf{k}{b}")
-            g = gain_sb[:, b, :].unsqueeze(1).unsqueeze(3).to_broadcast([P, W // 2, 4, 2])
-            nc.vector.tensor_tensor(woven_out(st), woven_in(th), g, ALU.mult)
-            z1_q[k, b] = quantise(st, f"z1_{k}{b}")
-
-        def gain_on_scalar(k, b, th):
-            n = PIECES[k][1]
-            flat = stage_tile(f"z1_flat{k}{b}", n)
-            for t in range(4):
-                nc.scalar.activation(flat[:, t * n : (t + 1) * n], th[:, t, :], ACT.Copy, scale=gain_sb[:, b, t : t + 1])
-            st = stage_tile(f"z1_bf{k}{b}", n)
-            nc.scalar.copy(woven_out(st, 4), flat[:].rearrange("p (i c e) -> p c i e", i=4, e=4))
-            return st
-
-        def later_piece(k):
-            j0, n = PIECES[k]
-            done = []
-            for b in range(2):
-                th = planes_tile(f"th{k}{b}", n)
-                for t in range(4):
-                    acc = bank(f"h_acc{k}{b}{t}", "h")
-                    first_product(acc[:], k, b, t)
-                    nc.scalar.activation(th[:, t, :], acc[:], ACT.Tanh)
-                    nc.scalar.copy(h1[4 * b + t][:, j0 : j0 + n], acc[:])
-                done.append(gain_on_scalar(k, b, th))
-            return done
-
-        def buyers_out(k, c, y=None):
-            j0, n = PIECES[k]
-            h, j = divmod(j0, W)
-            acc = bank(f"y1_acc{k}{c}", "y")
-            cols = slice(c * P, (c + 1) * P)
-            for a in (1, 0):
-                mx(acc[:, 0:n], w4_q[a][0][:, cols].bitcast(FP8X4), w4_q[a][1][:, cols],
-                   z1_q[k, a][0][:].bitcast(FP8X4), z1_q[k, a][1][:], a == 1, a == 0)
-            base = base_sb[c, h][:, j : j + n]
-            if y is None:
-                y = base
-            nc.vector.tensor_tensor(y, acc[:, 0:n], base, ALU.add)
-            part = offs3_sb[:, j0 // 16 : (j0 + n) // 16]
-            nc.vector.tensor_tensor(page[c][:].indirect(part), y, wg1_sb[h][:, j : j + n], ALU.mult)
-
+        z1_bf = stage_tile("z1_bf0", 2)
         accs = []
         for b in range(2):
             th = planes_tile(f"th0{b}")
             for t in range(4):
-                accs.append(bank(f"h_acc0{b}{t}", ("y", "h", "ha", "hb")[2 * b + t // 2]))
-                first_product(accs[-1][:], 0, b, t)
+                accs.append(first_product(0, b, t, ("y", "h", "ha", "hb")[2 * b + t // 2]))
                 nc.scalar.activation(th[:, t, :], accs[-1][:], ACT.Tanh)
-            gain_on_vector(0, b, th)
-        for r in range(2):
+            gains = gain_sb[:, b, :].unsqueeze(1).unsqueeze(3).to_broadcast([P, W // 2, 4, 2])
+            nc.vector.tensor_tensor(woven(operand(z1_bf, b), 2), to_weave(th[:], 2), gains, ALU.mult)
+        z1_q = [quantise(z1_bf, "z1_0")]
+        for r in range(8):
             nc.scalar.copy(h1[r][:, 0:W], accs[r][:])
 
-        w4_q = []
+        w4_bf = stage_tile("w4_bf", 2)
         for a in range(2):
-            st = stage_tile(f"w4_bf{a}")
-            nc.vector.tensor_copy(woven_out(st), woven_in(w4_raw[a]))
-            w4_q.append(quantise(st, f"w4_{a}"))
-        for r in range(2, 8):
-            nc.scalar.copy(h1[r][:, 0:W], accs[r][:])
+            nc.vector.tensor_copy(woven(operand(w4_bf, a), 2), to_weave(w4_raw[a][:], 2))
+        w4_q = quantise(w4_bf, "w4")
 
-        v2_s0 = held([P, W], U8, "v2_s0")
-        nc.vector.tensor_copy(v2_s0[:], tab2_s[:].indirect(offs2_sb[:]))
-        v2_w = []
+        v2_w = [held([P, NP], U32, f"v2_w{a}") for a in range(2)]
         for a in range(2):
-            v2_w.append(held([P, W], U32, f"v2_w{a}"))
             nc.vector.tensor_copy(v2_w[a][:], tab2_w[a][:].bitcast(U32).indirect(offs2_sb[:]))
-        v2_s1 = zeroed_bytes(W, "v2_s1")
-        nc.gpsimd.dma_start(v2_s1[0 : P - 4, :].bitcast(I32), v2_s0[4:P, :].bitcast(I32))
-        v2_s = [v2_s0, v2_s1]
+        v2 = [fp8((v2_w[a], v2_s[a]), 0, NP) for a in range(2)]
 
-        nc.sync.dma_start(wg1_sb[1][:], wg1[:, W:S])
-        w3_raw = {}
-
-        def load_w3(a, b):
-            w3_raw[a, b] = load_rows(w3[a * W : (a + 1) * W, b * W : (b + 1) * W], f"w3_raw{a}{b}")
-
-        load_w3(0, 0)
-        load_w3(1, 0)
+        w3_raw = {(a, 0): load_w3(a, 0) for a in range(2)}
+        w3_raw[0, 1] = load_w3(0, 1)
         load_base(0, 1)
         load_base(1, 1)
-        load_w3(0, 1)
-        load_w3(1, 1)
+        nc.sync.dma_start(wg1_sb[1][:], wg1[:, W:S])
+        w3_raw[1, 1] = load_w3(1, 1)
         for a in range(2):
             nc.sync.dma_start(w2_raw[a][:].bitcast(I32), w2_words[a].bitcast(I32))
         pos1_sb = load_list(pos1, "pos1_sb")
         load_base(2, 1)
         load_base(3, 1)
-        load_scale_rows(w5_s, w5_scales)
+        for q in range(4):
+            nc.sync.dma_start(
+                w5_s[32 * q : 32 * q + 4, :].bitcast(I32).rearrange("p (a c) -> p a c", a=2),
+                w5_scales[:, 4 * q : 4 * q + 4, :].bitcast(I32).rearrange("a r c -> r a c"),
+            )
         offs4_sb = load_list(offs4, "offs4_sb")
-        w5_w = held([P, 4 * N], U8, "w5_w")
         nc.sync.dma_start(w5_w[:].bitcast(I32).rearrange("p (a c) -> p a c", a=2), w5_words.bitcast(I32).rearrange("a p c -> p a c"))
-        wg2_sb = held([P, NP], F32, "wg2_sb")
         nc.sync.dma_start(wg2_sb[:], wg2)
 
+        def buyers_out(h, c, y):
+            acc = bank(f"y1_acc{h}{c}", "y")
+            product(acc, [(fp8(w4_q, a * N + c * P, P), fp8(z1_q[h], a * W, W)) for a in range(2)])
+            nc.vector.tensor_tensor(y, acc[:], base_sb[c, h][:], ALU.add)
+            nc.vector.tensor_tensor(page[c][:].indirect(offs3_sb[:, halves[h][1]]), y, wg1_sb[h][:], ALU.mult)
+
         for c in range(4):
-            buyers_out(0, c)
-        for b, st in enumerate(later_piece(1)):
-            z1_q[1, b] = quantise(st, f"z1_1{b}", f"base{2 * b + 1}_0")
+            buyers_out(0, c, base_sb[c, 0][:])
+
+        flats = [stage_tile("z1_flat0", 1)]
+        z1_bf = stage_tile("z1_bf1", 2)
+        flats.append(stage_tile("z1_flat1", 1))
+        for b in range(2):
+            th = planes_tile(f"th1{b}")
+            for t in range(4):
+                acc = first_product(1, b, t, "h")
+                nc.scalar.activation(th[:, t, :], acc[:], ACT.Tanh)
+                nc.scalar.copy(h1[4 * b + t][:, W:S], acc[:])
+            for t in range(4):
+                nc.scalar.activation(flats[b][:, t * W : (t + 1) * W], th[:, t, :], ACT.Copy, scale=gain_sb[:, b, t : t + 1])
+            nc.scalar.copy(woven(operand(z1_bf, b), 4), to_weave(flats[b][:].rearrange("p (i j) -> p i j", i=4), 4))
+        z1_q.append(quantise(z1_bf, "z1_1", codes_tag="v_w", scales_tag="base3_0"))
+
         for c in range(2):
-            buyers_out(1, c)
+            buyers_out(1, c, base_sb[c, 1][:])
+
+        w2_s0 = held([P, H], U8, "w2_s0")
+        nc.vector.tensor_copy(
+            w2_s0[:].rearrange("p (b t m) -> p b t m", b=2, t=4), w2_s_raw[:].rearrange("p (b m t) -> p b t m", b=2, t=4)
+        )
+        w2_s = [w2_s0, second_plane(w2_s0, "w2_s1")]
+
+        w3_q = []
+        for b in range(2):
+            w3_bf = stage_tile(f"w3_bf{b}", 2)
+            for a in range(2):
+                nc.scalar.copy(dealt(operand(w3_bf, a)), to_deal(w3_raw[a, b]))
+            w3_q.append(quantise(w3_bf, f"w3_{b}"))
 
         w2_w = [held([P, 2 * H], U8, f"w2_w{a}") for a in range(2)]
-        w2_s = held([P, 2 * H], U8, "w2_s")
-        nc.vector.tensor_copy(
-            w2_s[:].rearrange("p (g t m) -> p g t m", g=4, t=4),
-            w2_sraw[:].rearrange("p (g m t) -> p g t m", g=4, t=4),
-        )
-
-        w3_q = {}
-        z2_q = []
-
-        def quantise_w3(b):
-            for a in range(2):
-                w3_q[a, b] = quantise(round_dealt(w3_raw[a, b], f"w3_bf{a}{b}"), f"w3_{a}{b}")
-
-        def holders_stage(b):
-            z2 = planes_tile(f"z2_{b}")
-            for t in range(4):
-                ha = bank(f"ha{b}{t}", "ha")
-                hb = bank(f"hb{b}{t}", "hb")
-                cols = slice(t * P, (t + 1) * P)
-                for a in (1, 0):
-                    c0 = b * W + t * P
-                    mx(ha[:], w2_w[a][:, 2 * c0 : 2 * c0 + 2 * P].bitcast(FP4X4), w2_s[:, a * H + c0 : a * H + c0 + P],
-                       v2_w[a][:].bitcast(FP8X4), v2_s[a][:], a == 1, a == 0)
-                for a in (1, 0):
-                    mx(hb[:], w3_q[a, b][0][:, cols].bitcast(FP8X4), w3_q[a, b][1][:, cols],
-                       v2_w[a][:].bitcast(FP8X4), v2_s[a][:], a == 1, a == 0)
-                h2 = ring.tile([P, W], F32, name=f"h2_{b}{t}", tag="h2", bufs=4, align_bytes=64)
-                nc.scalar.copy(h2[:], ha[:])
-                nc.vector.tensor_tensor(h2[:], hb[:], h2[:], ALU.max)
-                nc.vector.tensor_tensor(z2[:, t, :], h1[4 * b + t][:].indirect(pos1_sb[:]), h2[:], ALU.mult)
-            st = stage_tile(f"z2_bf{b}")
-            nc.scalar.copy(woven_out(st), woven_in(z2))
-            z2_q.append(quantise(st, f"z2_{b}", f"qa{b}"))
-            return h2, z2
-
-        quantise_w3(0)
-        quantise_w3(1)
         for a in range(2):
             nc.scalar.copy(
                 w2_w[a][:].bitcast(U16).rearrange("p (b t m) -> p b t m", b=2, t=4),
                 w2_raw[a][:].bitcast(U16).rearrange("p (b m t) -> p b t m", b=2, t=4),
             )
-        holders_stage(0)
-        h2, z2 = holders_stage(1)
+
+        z2_bf = stage_tile("z2_bf", 2)
+        for b in range(2):
+            z2 = planes_tile(f"z2_{b}")
+            for t in range(4):
+                ha = bank(f"ha{b}{t}", "ha")
+                hb = bank(f"hb{b}{t}", "hb")
+                product(ha, [(fp4(w2_w[a], w2_s[a], b * W + t * P, P), v2[a]) for a in (1, 0)])
+                product(hb, [(fp8(w3_q[b], a * W + t * P, P), v2[a]) for a in range(2)])
+                h2 = row_tile(f"h2_{b}{t}")
+                nc.scalar.copy(h2[:], ha[:])
+                nc.vector.tensor_tensor(h2[:], hb[:], h2[:], ALU.max)
+                nc.vector.tensor_tensor(z2[:, t, :], h1[4 * b + t][:].indirect(pos1_sb[:]), h2[:], ALU.mult)
+            nc.scalar.copy(woven(operand(z2_bf, b), 2), to_weave(z2[:], 2))
+        z2_q = quantise(z2_bf, "z2", codes_tag="z1_0_codes")
+
         buyers_out(1, 2, h2[:])
         buyers_out(1, 3, z2[:, 0, :])
 
         for c in range(4):
             acc = bank(f"y2_acc{c}", "y")
-            for a in (1, 0):
-                c0 = a * N + c * P
-                mx(acc[:], w5_w[:, 2 * c0 : 2 * c0 + 2 * P].bitcast(FP4X4), w5_s[:, c0 : c0 + P],
-                   z2_q[a][0][:].bitcast(FP8X4), z2_q[a][1][:], a == 1, a == 0)
-            y2 = ring.tile([P, W], F32, name=f"y2_{c}", tag="h2", bufs=4, align_bytes=64)
+            product(acc, [(fp4(w5_w, w5_s, a * N + c * P, P), fp8(z2_q, a * W, W)) for a in range(2)])
+            y2 = row_tile(f"y2_{c}")
             nc.scalar.copy(y2[:], acc[:])
             nc.vector.tensor_tensor(page[c][:].indirect(offs4_sb[:]), y2[:], wg2_sb[:], ALU.mult)
             nc.sync.dma_start(out[c * P : (c + 1) * P, :], page[c][:])

@@ -75,7 +75,7 @@ def tile_list_buyer_limit_features_kernel(
 
         def second_plane(stacked, name):
             tile = zeroed_bytes(stacked.shape[1], name)
-            nc.gpsimd.dma_start(tile[0 : P - 4, :].bitcast(I32), stacked[4:P, :].bitcast(I32))
+            nc.sync.dma_start(tile[0:112, :].bitcast(I32), stacked[4:116, :].bitcast(I32))
             return tile
 
         def operand(stage, a):
@@ -139,8 +139,8 @@ def tile_list_buyer_limit_features_kernel(
         tab_w = load_words(tab_words[0], "tab_w")
         offs2_sb = load_list(offs2, "offs2_sb")
         w1_raw = [load_rows(w1[:, b * W : (b + 1) * W], f"w1_raw{b}") for b in range(2)]
-        w4_raw = [load_rows(w4[0:W, :], "w4_raw0")]
         load_stacked_planes(tab2_s, tab2_scales)
+        w4_raw = [load_rows(w4[0:W, :], "w4_raw0")]
         nc.sync.dma_start(gain_sb[:], gain.rearrange("(b p t) -> p b t", b=2, t=4))
         w4_raw.append(load_rows(w4[W:H, :], "w4_raw1"))
         load_stacked_planes(w2_s_raw, w2_scales)
@@ -162,12 +162,12 @@ def tile_list_buyer_limit_features_kernel(
         for cols, entries in halves:
             nc.vector.tensor_copy(v_w[:, cols], tab_w[:].bitcast(U32).indirect(offs_sb[:, entries]))
 
-        w1_bf = [stage_tile(f"w1_bf{b}", 1) for b in range(2)]
-        nc.scalar.copy(dealt(w1_bf[0][:])[:, 0], to_deal(w1_raw[0])[:, 0])
-        nc.vector.tensor_copy(dealt(w1_bf[0][:])[:, 1], to_deal(w1_raw[0])[:, 1])
-        w1_q = [quantise(w1_bf[0], "w1_0")]
-        nc.vector.tensor_copy(dealt(w1_bf[1][:]), to_deal(w1_raw[1]))
-        w1_q.append(quantise(w1_bf[1], "w1_1"))
+        w1_bf = stage_tile("w1_bf", 1)
+        nc.scalar.copy(dealt(w1_bf[:])[:, 0], to_deal(w1_raw[0])[:, 0])
+        nc.vector.tensor_copy(dealt(w1_bf[:])[:, 1], to_deal(w1_raw[0])[:, 1])
+        w1_q = [quantise(w1_bf, "w1_0")]
+        nc.vector.tensor_copy(dealt(w1_bf[:]), to_deal(w1_raw[1]))
+        w1_q.append(quantise(w1_bf, "w1_1"))
 
         v2_s0 = held([P, NP], U8, "v2_s0")
         nc.vector.tensor_copy(v2_s0[:], tab2_s[:].indirect(offs2_sb[:]))
@@ -180,7 +180,9 @@ def tile_list_buyer_limit_features_kernel(
             product(acc, [(fp8(w1_q[b], t * P, P), fp8((v_w, v_s), h * W, W))])
             return acc
 
-        z1_bf = stage_tile("z1_bf0", 2)
+        w4_bf = stage_tile("w4_bf", 2)
+        nc.vector.tensor_copy(woven(operand(w4_bf, 0), 2), to_weave(w4_raw[0][:], 2))
+        z1_bf = w4_raw[0][:].rearrange("p i c -> p (i c)").bitcast(BF16)
         accs = []
         for b in range(2):
             th = planes_tile(f"th0{b}")
@@ -193,9 +195,7 @@ def tile_list_buyer_limit_features_kernel(
         for r in range(8):
             nc.scalar.copy(h1[r][:, 0:W], accs[r][:])
 
-        w4_bf = stage_tile("w4_bf", 2)
-        for a in range(2):
-            nc.vector.tensor_copy(woven(operand(w4_bf, a), 2), to_weave(w4_raw[a][:], 2))
+        nc.vector.tensor_copy(woven(operand(w4_bf, 1), 2), to_weave(w4_raw[1][:], 2))
         w4_q = quantise(w4_bf, "w4")
 
         v2_w = [held([P, NP], U32, f"v2_w{a}") for a in range(2)]
@@ -223,11 +223,17 @@ def tile_list_buyer_limit_features_kernel(
         nc.sync.dma_start(w5_w[:].bitcast(I32).rearrange("p (a c) -> p a c", a=2), w5_words.bitcast(I32).rearrange("a p c -> p a c"))
         nc.sync.dma_start(wg2_sb[:], wg2)
 
-        def buyers_out(h, c, y):
+        def buyers_sum(h, c, y):
             acc = bank(f"y1_acc{h}{c}", "y")
             product(acc, [(fp8(w4_q, a * N + c * P, P), fp8(z1_q[h], a * W, W)) for a in range(2)])
             nc.vector.tensor_tensor(y, acc[:], base_sb[c, h][:], ALU.add)
+
+        def buyers_put(h, c, y):
             nc.vector.tensor_tensor(page[c][:].indirect(offs3_sb[:, halves[h][1]]), y, wg1_sb[h][:], ALU.mult)
+
+        def buyers_out(h, c, y):
+            buyers_sum(h, c, y)
+            buyers_put(h, c, y)
 
         for c in range(4):
             buyers_out(0, c, base_sb[c, 0][:])
@@ -238,7 +244,7 @@ def tile_list_buyer_limit_features_kernel(
         for b in range(2):
             th = planes_tile(f"th1{b}")
             for t in range(4):
-                acc = first_product(1, b, t, "h")
+                acc = first_product(1, b, t, ("h", "ha", "hb", "h")[2 * b + t // 2])
                 nc.scalar.activation(th[:, t, :], acc[:], ACT.Tanh)
                 nc.scalar.copy(h1[4 * b + t][:, W:S], acc[:])
             for t in range(4):
@@ -270,8 +276,10 @@ def tile_list_buyer_limit_features_kernel(
             )
 
         z2_bf = stage_tile("z2_bf", 2)
+        z2s = []
         for b in range(2):
             z2 = planes_tile(f"z2_{b}")
+            z2s.append(z2)
             for t in range(4):
                 ha = bank(f"ha{b}{t}", "ha")
                 hb = bank(f"hb{b}{t}", "hb")
@@ -281,11 +289,12 @@ def tile_list_buyer_limit_features_kernel(
                 nc.scalar.copy(h2[:], ha[:])
                 nc.vector.tensor_tensor(h2[:], hb[:], h2[:], ALU.max)
                 nc.vector.tensor_tensor(z2[:, t, :], h1[4 * b + t][:].indirect(pos1_sb[:]), h2[:], ALU.mult)
-            nc.scalar.copy(woven(operand(z2_bf, b), 2), to_weave(z2[:], 2))
-        z2_q = quantise(z2_bf, "z2", codes_tag="z1_0_codes")
-
+        for b in range(2):
+            nc.scalar.copy(woven(operand(z2_bf, b), 2), to_weave(z2s[b][:], 2))
         buyers_out(1, 2, h2[:])
-        buyers_out(1, 3, z2[:, 0, :])
+        buyers_sum(1, 3, z2[:, 0, :])
+        z2_q = quantise(z2_bf, "z2", codes_tag="z1_0_codes")
+        buyers_put(1, 3, z2[:, 0, :])
 
         for c in range(4):
             acc = bank(f"y2_acc{c}", "y")

from contextlib import ExitStack

import concourse.mybir as mybir

T, S, NP, T2, K, K2, H, N = 2048, 1024, 512, 2048, 512, 1024, 1024, 512
FLOPS = 2 * (K * H * S + 2 * K2 * H * NP + H * N * S + H * N * NP)

F32 = mybir.dt.float32
BF16 = mybir.dt.bfloat16
I32 = mybir.dt.int32
U32 = mybir.dt.uint32
U16 = mybir.dt.uint16
U8 = mybir.dt.uint8
FP8X4 = mybir.dt.float8_e4m3fn_x4
FP4X4 = mybir.dt.float4_e2m1fn_x4
ALU = mybir.AluOpType
ACT = mybir.ActivationFunctionType

P = 128
W = 512


def tile_list_buyer_limit_features_kernel(
    tc, tab_words, tab_scales, tab2_words, tab2_scales, offs, offs2, pos1, offs3, offs4, w1, w2_words, w2_scales, w3,
    gain, w4, w5_words, w5_scales, base1, page1, wg1, wg2, out
):
    nc = tc.nc
    with ExitStack() as ctx:
        lists = ctx.enter_context(tc.tile_pool(name="lists", bufs=1))
        keep = ctx.enter_context(tc.tile_pool(name="keep", bufs=1))
        ring = ctx.enter_context(tc.tile_pool(name="ring", bufs=1))
        psum = ctx.enter_context(tc.psum_pool(name="psum", bufs=1))

        def held(shape, dtype, name, tag=None):
            return keep.tile(shape, dtype, name=name, tag=tag or name, align_bytes=64)

        def raw_tile(shape, dtype, name):
            return ring.tile(shape, dtype, name=name, tag="raw", bufs=6, align_bytes=64)

        def stage_tile(name, operands):
            return ring.tile([P, operands * 4 * W], BF16, name=name, tag="stage", bufs=3, align_bytes=64)

        def planes_tile(name):
            return ring.tile([P, 4, W], F32, name=name, tag="planes", bufs=2, align_bytes=64)

        def row_tile(name):
            return ring.tile([P, W], F32, name=name, tag="row", bufs=4, align_bytes=64)

        def bank(name, tag):
            return psum.tile([P, W], F32, name=name, tag=tag, bufs=2)

        def zeroed_bytes(cols, name):
            tile = held([P, cols], U8, name)
            nc.vector.memset(tile[:].bitcast(I32), 0)
            return tile

        def load_list(src, name):
            tile = lists.tile([P, src.shape[1]], U16, name=name)
            nc.sync.dma_start(tile[:], src)
            return tile

        def load_words(src, name):
            tile = raw_tile([P, T], I32, name)
            nc.sync.dma_start(tile[:], src.rearrange("p t i -> p (t i)").bitcast(I32))
            return tile

        def load_rows(src, name):
            tile = raw_tile([P, 4, W], F32, name)
            nc.sync.dma_start(tile[:], src.rearrange("(p i) c -> p i c", i=4))
            return tile

        def load_stacked_planes(tile, src):
            for q in range(4):
                nc.sync.dma_start(tile[32 * q : 32 * q + 8, :].bitcast(I32), src[:, 4 * q : 4 * q + 4, :].bitcast(I32))

        def second_plane(stacked, name):
            tile = zeroed_bytes(stacked.shape[1], name)
            nc.sync.dma_start(tile[0:112, :].bitcast(I32), stacked[4:116, :].bitcast(I32))
            return tile

        def operand(stage, a):
            return stage[:, a * 4 * W : (a + 1) * 4 * W]

        def dealt(bf):
            return bf.rearrange("p (u v m i) -> p u m i v", u=2, v=2, i=4)

        def to_deal(raw):
            return raw[:].rearrange("p i (m u v) -> p u m i v", u=2, v=2)

        def woven(bf, e):
            return bf.rearrange("p (c e i) -> p c i e", e=e, i=4)

        def to_weave(planes, e):
            return planes.rearrange("p i (c e) -> p c i e", e=e)

        def quantise(stage, name, codes_tag=None, scales_tag=None):
            cols = stage.shape[1] // 4
            codes = held([P, cols], U32, name + "_codes", codes_tag)
            scales = held([P, cols], U8, name + "_scales", scales_tag)
            nc.vector.quantize_mx(out=codes[:].bitcast(FP8X4), scales=scales[:], in_=stage[:])
            return codes, scales

        def fp8(quantised, c0, n):
            return quantised[0][:, c0 : c0 + n].bitcast(FP8X4), quantised[1][:, c0 : c0 + n]

        def fp4(words, scales, c0, n):
            return words[:, 2 * c0 : 2 * (c0 + n)].bitcast(FP4X4), scales[:, c0 : c0 + n]

        def product(acc, passes):
            for n, (lhs, rhs) in enumerate(passes):
                nc.tensor.matmul_mx(out=acc[:], lhsT=lhs[0], lhsT_scale=lhs[1], rhs=rhs[0], rhs_scale=rhs[1],
                                    start=n == 0, stop=n == len(passes) - 1)

        tab2_s = zeroed_bytes(T, "tab2_s")
        w2_s_raw = zeroed_bytes(H, "w2_s_raw")
        w5_s = zeroed_bytes(2 * N, "w5_s")
        tab_s = held([P, T], U8, "tab_s")
        gain_sb = held([P, 2, 4], F32, "gain_sb")
        wg1_sb = [held([P, W], F32, f"wg1_sb{h}") for h in range(2)]
        wg2_sb = held([P, NP], F32, "wg2_sb")
        base_sb = {(c, h): held([P, W], F32, f"base{c}_{h}") for c in range(4) for h in range(2)}
        page = [held([P, T2], F32, f"page{c}") for c in range(4)]
        w2_raw = [held([P, 2 * H], U8, f"w2_raw{a}") for a in range(2)]
        w5_w = held([P, 4 * N], U8, "w5_w")

        def load_base(c, h):
            nc.sync.dma_start(base_sb[c, h][:], base1[c * P : (c + 1) * P, h * W : (h + 1) * W])

        def load_page(c):
            nc.sync.dma_start(page[c][:], page1[c * P : (c + 1) * P, :])

        def load_w3(a, b):
            return load_rows(w3[a * W : (a + 1) * W, b * W : (b + 1) * W], f"w3_raw{a}{b}")

        offs_sb = load_list(offs, "offs_sb")
        for q in range(4):
            rows = tab_scales[0, 4 * q : 4 * q + 4, :].bitcast(I32)
            nc.sync.dma_start(tab_s[32 * q : 32 * q + 32, :].bitcast(I32), rows.unsqueeze(0).to_broadcast([8, 4, T // 4]))
        tab_w = load_words(tab_words[0], "tab_w")
        offs2_sb = load_list(offs2, "offs2_sb")
        w1_raw = [load_rows(w1[:, b * W : (b + 1) * W], f"w1_raw{b}") for b in range(2)]
        load_stacked_planes(tab2_s, tab2_scales)
        w4_raw = [load_rows(w4[0:W, :], "w4_raw0")]
        nc.sync.dma_start(gain_sb[:], gain.rearrange("(b p t) -> p b t", b=2, t=4))
        w4_raw.append(load_rows(w4[W:H, :], "w4_raw1"))
        load_stacked_planes(w2_s_raw, w2_scales)
        offs3_sb = load_list(offs3, "offs3_sb")
        tab2_w = [load_words(tab2_words[0], "tab2_w0")]
        nc.sync.dma_start(wg1_sb[0][:], wg1[:, 0:W])
        load_base(0, 0)
        for c in range(3):
            load_base(c + 1, 0)
            load_page(c)
        tab2_w.append(load_words(tab2_words[1], "tab2_w1"))
        load_page(3)

        v_w = held([P, S], U32, "v_w")
        v_s = held([P, S], U8, "v_s")
        halves = [(slice(h * W, (h + 1) * W), slice(h * W // 16, (h + 1) * W // 16)) for h in range(2)]
        for cols, entries in halves:
            nc.vector.tensor_copy(v_s[:, cols], tab_s[:].indirect(offs_sb[:, entries]))
        for cols, entries in halves:
            nc.vector.tensor_copy(v_w[:, cols], tab_w[:].bitcast(U32).indirect(offs_sb[:, entries]))

        w1_bf = stage_tile("w1_bf", 1)
        nc.scalar.copy(dealt(w1_bf[:])[:, 0], to_deal(w1_raw[0])[:, 0])
        nc.vector.tensor_copy(dealt(w1_bf[:])[:, 1], to_deal(w1_raw[0])[:, 1])
        w1_q = [quantise(w1_bf, "w1_0")]
        nc.vector.tensor_copy(dealt(w1_bf[:]), to_deal(w1_raw[1]))
        w1_q.append(quantise(w1_bf, "w1_1"))

        v2_s0 = held([P, NP], U8, "v2_s0")
        nc.vector.tensor_copy(v2_s0[:], tab2_s[:].indirect(offs2_sb[:]))
        v2_s = [v2_s0, second_plane(v2_s0, "v2_s1")]

        h1 = [held([P, S], F32, f"h1_{r}") for r in range(8)]

        def first_product(h, b, t, tag):
            acc = bank(f"h_acc{h}{b}{t}", tag)
            product(acc, [(fp8(w1_q[b], t * P, P), fp8((v_w, v_s), h * W, W))])
            return acc

        w4_bf = stage_tile("w4_bf", 2)
        nc.vector.tensor_copy(woven(operand(w4_bf, 0), 2), to_weave(w4_raw[0][:], 2))
        z1_bf = w4_raw[0][:].rearrange("p i c -> p (i c)").bitcast(BF16)
        accs = []
        for b in range(2):
            th = planes_tile(f"th0{b}")
            for t in range(4):
                accs.append(first_product(0, b, t, ("y", "h", "ha", "hb")[2 * b + t // 2]))
                nc.scalar.activation(th[:, t, :], accs[-1][:], ACT.Tanh)
            gains = gain_sb[:, b, :].unsqueeze(1).unsqueeze(3).to_broadcast([P, W // 2, 4, 2])
            nc.vector.tensor_tensor(woven(operand(z1_bf, b), 2), to_weave(th[:], 2), gains, ALU.mult)
        z1_q = [quantise(z1_bf, "z1_0")]
        for r in range(8):
            nc.scalar.copy(h1[r][:, 0:W], accs[r][:])

        nc.vector.tensor_copy(woven(operand(w4_bf, 1), 2), to_weave(w4_raw[1][:], 2))
        w4_q = quantise(w4_bf, "w4")

        v2_w = [held([P, NP], U32, f"v2_w{a}") for a in range(2)]
        for a in range(2):
            nc.vector.tensor_copy(v2_w[a][:], tab2_w[a][:].bitcast(U32).indirect(offs2_sb[:]))
        v2 = [fp8((v2_w[a], v2_s[a]), 0, NP) for a in range(2)]

        w3_raw = {(a, 0): load_w3(a, 0) for a in range(2)}
        w3_raw[0, 1] = load_w3(0, 1)
        load_base(0, 1)
        load_base(1, 1)
        nc.sync.dma_start(wg1_sb[1][:], wg1[:, W:S])
        w3_raw[1, 1] = load_w3(1, 1)
        for a in range(2):
            nc.sync.dma_start(w2_raw[a][:].bitcast(I32), w2_words[a].bitcast(I32))
        pos1_sb = load_list(pos1, "pos1_sb")
        load_base(2, 1)
        load_base(3, 1)
        for q in range(4):
            nc.sync.dma_start(
                w5_s[32 * q : 32 * q + 4, :].bitcast(I32).rearrange("p (a c) -> p a c", a=2),
                w5_scales[:, 4 * q : 4 * q + 4, :].bitcast(I32).rearrange("a r c -> r a c"),
            )
        offs4_sb = load_list(offs4, "offs4_sb")
        nc.sync.dma_start(w5_w[:].bitcast(I32).rearrange("p (a c) -> p a c", a=2), w5_words.bitcast(I32).rearrange("a p c -> p a c"))
        nc.sync.dma_start(wg2_sb[:], wg2)

        def buyers_sum(h, c, y):
            acc = bank(f"y1_acc{h}{c}", "y")
            product(acc, [(fp8(w4_q, a * N + c * P, P), fp8(z1_q[h], a * W, W)) for a in range(2)])
            nc.vector.tensor_tensor(y, acc[:], base_sb[c, h][:], ALU.add)

        def buyers_put(h, c, y):
            nc.vector.tensor_tensor(page[c][:].indirect(offs3_sb[:, halves[h][1]]), y, wg1_sb[h][:], ALU.mult)

        def buyers_out(h, c, y):
            buyers_sum(h, c, y)
            buyers_put(h, c, y)

        for c in range(4):
            buyers_out(0, c, base_sb[c, 0][:])

        flats = [stage_tile("z1_flat0", 1)]
        z1_bf = stage_tile("z1_bf1", 2)
        flats.append(stage_tile("z1_flat1", 1))
        for b in range(2):
            th = planes_tile(f"th1{b}")
            for t in range(4):
                acc = first_product(1, b, t, ("h", "ha", "hb", "h")[2 * b + t // 2])
                nc.scalar.activation(th[:, t, :], acc[:], ACT.Tanh)
                nc.scalar.copy(h1[4 * b + t][:, W:S], acc[:])
            for t in range(4):
                nc.scalar.activation(flats[b][:, t * W : (t + 1) * W], th[:, t, :], ACT.Copy, scale=gain_sb[:, b, t : t + 1])
            nc.scalar.copy(woven(operand(z1_bf, b), 4), to_weave(flats[b][:].rearrange("p (i j) -> p i j", i=4), 4))
        z1_q.append(quantise(z1_bf, "z1_1", codes_tag="v_w", scales_tag="base3_0"))

        for c in range(2):
            buyers_out(1, c, base_sb[c, 1][:])

        w2_s0 = held([P, H], U8, "w2_s0")
        nc.vector.tensor_copy(
            w2_s0[:].rearrange("p (b t m) -> p b t m", b=2, t=4), w2_s_raw[:].rearrange("p (b m t) -> p b t m", b=2, t=4)
        )
        w2_s = [w2_s0, second_plane(w2_s0, "w2_s1")]

        w3_q = []
        for b in range(2):
            w3_bf = stage_tile(f"w3_bf{b}", 2)
            for a in range(2):
                nc.scalar.copy(dealt(operand(w3_bf, a)), to_deal(w3_raw[a, b]))
            w3_q.append(quantise(w3_bf, f"w3_{b}"))

        w2_w = [held([P, 2 * H], U8, f"w2_w{a}") for a in range(2)]
        for a in range(2):
            nc.scalar.copy(
                w2_w[a][:].bitcast(U16).rearrange("p (b t m) -> p b t m", b=2, t=4),
                w2_raw[a][:].bitcast(U16).rearrange("p (b m t) -> p b t m", b=2, t=4),
            )

        z2_bf = stage_tile("z2_bf", 2)
        z2s = []
        for b in range(2):
            z2 = planes_tile(f"z2_{b}")
            z2s.append(z2)
            for t in range(4):
                ha = bank(f"ha{b}{t}", "ha")
                hb = bank(f"hb{b}{t}", "hb")
                product(ha, [(fp4(w2_w[a], w2_s[a], b * W + t * P, P), v2[a]) for a in (1, 0)])
                product(hb, [(fp8(w3_q[b], a * W + t * P, P), v2[a]) for a in range(2)])
                h2 = row_tile(f"h2_{b}{t}")
                nc.scalar.copy(h2[:], ha[:])
                nc.vector.tensor_tensor(h2[:], hb[:], h2[:], ALU.max)
                nc.vector.tensor_tensor(z2[:, t, :], h1[4 * b + t][:].indirect(pos1_sb[:]), h2[:], ALU.mult)
        for b in range(2):
            nc.scalar.copy(woven(operand(z2_bf, b), 2), to_weave(z2s[b][:], 2))
        buyers_out(1, 2, h2[:])
        buyers_sum(1, 3, z2[:, 0, :])
        z2_q = quantise(z2_bf, "z2", codes_tag="z1_0_codes")
        buyers_put(1, 3, z2[:, 0, :])

        for c in range(4):
            acc = bank(f"y2_acc{c}", "y")
            product(acc, [(fp4(w5_w, w5_s, a * N + c * P, P), fp8(z2_q, a * W, W)) for a in range(2)])
            y2 = row_tile(f"y2_{c}")
            nc.scalar.copy(y2[:], acc[:])
            nc.vector.tensor_tensor(page[c][:].indirect(offs4_sb[:]), y2[:], wg2_sb[:], ALU.mult)
            nc.sync.dma_start(out[c * P : (c + 1) * P, :], page[c][:])
